import numpy as np
import ml_dtypes


def mxq(x, axis, fmt="e4m3"):
    dtype, down = {"e4m3": (ml_dtypes.float8_e4m3fn, 7), "e5m2": (ml_dtypes.float8_e5m2, 14)}[fmt]
    v = np.moveaxis(np.asarray(x, np.float32).astype(ml_dtypes.bfloat16).astype(np.float64), axis, -1)
    blocks = v.reshape(v.shape[:-1] + (-1, 32))
    amax = np.abs(blocks).max(-1, keepdims=True)
    byte = np.maximum(np.where(amax > 0, np.frexp(amax)[1] - 1 + 127, 0) - down, 1)
    scale = np.exp2(byte - 127.0)
    codes = (blocks / scale).astype(np.float32).astype(dtype).astype(np.float64)
    return np.moveaxis((codes * scale).reshape(v.shape), -1, axis)


WIDE = False


def mx_kscale(k):
    if not WIDE:
        return np.ones(k)
    levels = np.array([10, -10, 5, -5, 0])
    if k % 512:
        return np.exp2(np.random.permutation(np.resize(levels, k // 32))).repeat(32)
    a = np.empty((k // 512, 16))
    for p in range(k // 512):
        a[p, :8] = np.random.permutation(np.resize(levels, 8))
        for g in range(8):
            far = levels[np.abs(levels - a[p, g]) >= 10]
            a[p, g + 8] = far[np.random.randint(len(far))]
    return np.exp2(a.ravel()).repeat(32)


def f64(x):
    return np.asarray(x).astype(np.float64)


def striped(idx):
    return np.tile(idx.reshape(-1, 16).T, (8, 1)).astype(np.uint16)


def unstriped(offs):
    return offs[:16].T.reshape(-1).astype(np.int64)


def striped8(idx):
    return np.concatenate([x.reshape(-1, 16).T for x in idx]).astype(np.uint16)


def runs(offs, k):
    lists = np.stack([offs[16 * r : 16 * r + 16].T.reshape(-1) for r in range(8)]).astype(np.int64)
    return lists[np.arange(k) % 512 // 64]


def pack_weight(w):
    k, n = w.shape
    w = f64(np.asarray(w, np.float32).astype(ml_dtypes.bfloat16)).reshape(k // 32, 32, n)
    amax = np.abs(w).max(1)
    byte = np.clip(np.where(amax > 0, np.frexp(amax)[1] - 1 + 127 - 7, 1), 1, 254)
    scaled = (w * np.exp2(127.0 - byte)[:, None, :]).reshape(k, n).astype(np.float32)
    words = np.ascontiguousarray(scaled.reshape(k // 512, 128, 4, n).transpose(0, 1, 3, 2)).astype(ml_dtypes.float8_e4m3fn).view(np.uint8)
    return words, np.ascontiguousarray(byte.astype(np.uint8).reshape(k // 512, 16, n))


def unpack_weight(words, scales):
    g, p, n, _ = words.shape
    vals = np.ascontiguousarray(words).view(ml_dtypes.float8_e4m3fn).astype(np.float64) * np.repeat(np.exp2(scales.astype(np.float64) - 127.0), 8, axis=1)[..., None]
    return vals.transpose(0, 1, 3, 2).reshape(g * 512, n)


E2M1 = np.array([0.0, 0.5, 1.0, 1.5, 2.0, 3.0, 4.0, 6.0, -0.0, -0.5, -1.0, -1.5, -2.0, -3.0, -4.0, -6.0])


def pack_fp4(w):
    k, n = w.shape
    w = f64(np.asarray(w, np.float32).astype(ml_dtypes.bfloat16)).reshape(k // 32, 32, n)
    amax = np.abs(w).max(1)
    mant, ex = np.frexp(amax / 6.0)
    byte = np.clip(np.where(amax > 0, np.where(mant > 0.5, ex, ex - 1) + 127, 1), 1, 254)
    scaled = (w * np.exp2(127.0 - byte)[:, None, :]).reshape(k, n).astype(np.float32)
    c = np.ascontiguousarray(scaled.reshape(k // 512, 128, 4, n).transpose(0, 1, 3, 2)).astype(ml_dtypes.float4_e2m1fn).view(np.uint8) & 0xF
    words = (c[..., 0::2] | (c[..., 1::2] << 4)).reshape(k // 512, 128, 2 * n)
    return np.ascontiguousarray(words), np.ascontiguousarray(byte.astype(np.uint8).reshape(k // 512, 16, n))


def unpack_fp4(words, scales):
    g, _, n = scales.shape
    words = np.ascontiguousarray(words).reshape(g, 128, n, 2)
    nib = np.empty((g, 128, n, 4), np.uint8)
    nib[..., 0::2] = words & 0xF
    nib[..., 1::2] = words >> 4
    vals = E2M1[nib] * np.repeat(np.exp2(scales.astype(np.float64) - 127.0), 8, axis=1)[..., None]
    return vals.transpose(0, 1, 3, 2).reshape(g * 512, n)


def planes(y):
    n, m = y.shape
    v = y.astype(np.float32).astype(ml_dtypes.bfloat16).astype(np.float64).reshape(n // 32, 32, m)
    top = np.abs(v).max(1)
    byte = np.clip(np.where(top > 0, np.frexp(top)[1] - 1 + 127 - 7, 1), 1, 254)
    codes = (v * np.exp2(127.0 - byte)[:, None, :]).reshape(n, m).astype(np.float32).astype(ml_dtypes.float8_e4m3fn).view(np.uint8)
    words = codes.reshape(n // 512, 128, 4, m).transpose(0, 1, 3, 2)
    return np.ascontiguousarray(words), np.ascontiguousarray(byte.astype(np.uint8).reshape(n // 512, 16, m))


K, T, S, H, G = 512, 1024, 512, 512, 2048


def setup_inputs():
    n = np.random.standard_normal
    s = mx_kscale(K)[:, None]
    packed_xT = pack_weight(n((K, T)) * s)
    packed_w1 = pack_fp4(n((K, H)) / np.sqrt(K) / s)
    packed_w2 = pack_fp4(n((K, H)) / np.sqrt(K) / s)
    packed_dT = pack_weight(n((K, G)) / s)
    return {
        "x_words": packed_xT[0],
        "x_scales": packed_xT[1],
        "w1_words": packed_w1[0],
        "w1_scales": packed_w1[1],
        "w2_words": packed_w2[0],
        "w2_scales": packed_w2[1],
        "gs": (np.random.uniform(0.5, 1.5, (K, 1)) * s).astype(np.float32),
        "d_words": packed_dT[0],
        "d_scales": packed_dT[1],
        "offs": striped(np.random.permutation(T)[:S]),
        "two": striped(np.random.permutation(T)[:S]),
        "n1": striped8(np.stack([np.random.permutation(S) for _ in range(8)])),
        "n2": striped8(np.stack([np.random.permutation(S) for _ in range(8)])),
        "k1": striped8(np.random.randint(0, G, (8, H))),
        "n3": striped8(np.stack([np.random.permutation(S) for _ in range(8)])),
        "n4": striped8(np.stack([np.random.permutation(S) for _ in range(8)])),
        "n5": striped8(np.stack([np.random.permutation(S) for _ in range(8)])),
    }


def reference(x_words, x_scales, w1_words, w1_scales, w2_words, w2_scales, gs, d_words, d_scales, offs, two, n1, n2, k1, n3, n4, n5):
    d_k1 = unpack_weight(d_words, d_scales)[np.arange(K)[:, None], runs(k1, K)]
    xq = unpack_weight(x_words, x_scales)[:, unstriped(offs)]
    y = unpack_fp4(w1_words, w1_scales).T @ xq
    x_two = unpack_weight(x_words, x_scales)[:, unstriped(two)]
    d = unpack_fp4(w2_words, w2_scales).T @ x_two
    z = f64(gs) * (y[np.arange(H)[:, None], runs(n1, H)] - (np.tanh(d) * (d[np.arange(H)[:, None], runs(n2, H)])))
    h = 0.0625 * ((d_k1.T @ mxq(z, 0, "e4m3")))
    ex = np.exp(0.5 * h)
    out_0 = np.log((ex + ex[np.arange(H)[:, None], runs(n3, H)]) / (ex[np.arange(H)[:, None], runs(n4, H)] + ex[np.arange(H)[:, None], runs(n5, H)]))
    return (out_0,) + planes(out_0)

@@ -1,0 +1,217 @@
+from contextlib import ExitStack
+
+import concourse.mybir as mybir
+
+F32 = mybir.dt.float32
+BF16 = mybir.dt.bfloat16
+I32 = mybir.dt.int32
+U32 = mybir.dt.uint32
+U16 = mybir.dt.uint16
+U8 = mybir.dt.uint8
+FP8X4 = mybir.dt.float8_e4m3fn_x4
+FP4X4 = mybir.dt.float4_e2m1fn_x4
+ACT = mybir.ActivationFunctionType
+ALU = mybir.AluOpType
+
+P = 128
+PACK = 4
+K, T, S, H, G = 512, 1024, 512, 512, 2048
+HALF = S // 2
+LIST_COLS = S // 16
+FLOPS = 3 * 2 * K * H * S
+
+
+def tile_picked_twqsoftbodds_none_po_kernel(
+    tc, x_words, x_scales, w1_words, w1_scales, w2_words, w2_scales, gs, d_words, d_scales,
+    offs, two, n1, n2, k1, n3, n4, n5, out_0, out_1, out_2,
+):
+    nc = tc.nc
+    with ExitStack() as ctx:
+        lists = ctx.enter_context(tc.tile_pool(name="lists", bufs=1))
+        keep = ctx.enter_context(tc.tile_pool(name="keep", bufs=1))
+        psum = ctx.enter_context(tc.psum_pool(name="psum", bufs=1))
+
+        def sb(name, shape, dtype):
+            return keep.tile(shape, dtype, name=name, align_bytes=64)
+
+        def load_list(name, src):
+            tile = lists.tile([P, LIST_COLS], U16, name=name)
+            nc.sync.dma_start(tile[:], src)
+            return tile
+
+        def half_of(lst, h):
+            return lst[:, h * (LIST_COLS // 2) : (h + 1) * (LIST_COLS // 2)]
+
+        def load_scale_rows(queue, dst, src):
+            for q in range(4):
+                queue.dma_start(dst[32 * q : 32 * q + 4, :].bitcast(I32), src[0, 4 * q : 4 * q + 4, :].bitcast(I32))
+
+        xs_tab = sb("xs_tab", [P, T], U8)
+        w2s_raw = sb("w2s_raw", [P, H], U8)
+        w1s_raw = sb("w1s_raw", [P, H], U8)
+        ds_tab = sb("ds_tab", [P, G], U8)
+        nc.vector.memset(xs_tab[:].bitcast(I32), 0)
+        nc.vector.memset(w2s_raw[:].bitcast(I32), 0)
+        nc.gpsimd.memset(w1s_raw[:].bitcast(I32), 0)
+        nc.gpsimd.memset(ds_tab[:].bitcast(I32), 0)
+        z_scales = [sb("z_scales%d" % h, [P, HALF], U8) for h in range(2)]
+        for h in range(2):
+            nc.gpsimd.memset(z_scales[h][:].bitcast(I32), 0)
+
+        w2w_raw = sb("w2w_raw", [P, 2 * H], U8)
+        nc.sync.dma_start(w2w_raw[:].bitcast(I32), w2_words[0].bitcast(I32))
+        w1w_raw = sb("w1w_raw", [P, 2 * H], U8)
+        nc.scalar.dma_start(w1w_raw[:].bitcast(I32), w1_words[0].bitcast(I32))
+        two_l = load_list("two_l", two)
+        xw_tab = sb("xw_tab", [P, T], I32)
+        nc.sync.dma_start(xw_tab[:], x_words[0].rearrange("p n r -> p (n r)").bitcast(I32))
+        load_scale_rows(nc.scalar, xs_tab, x_scales)
+        offs_l = load_list("offs_l", offs)
+        load_scale_rows(nc.scalar, w2s_raw, w2_scales)
+        k1_l = load_list("k1_l", k1)
+        dw_tab = sb("dw_tab", [P, G], I32)
+        nc.sync.dma_start(dw_tab[:], d_words[0].rearrange("p n r -> p (n r)").bitcast(I32))
+        gain = sb("gain", [P, PACK], F32)
+        nc.sync.dma_start(gain[:], gs.rearrange("(p t) o -> p (t o)", t=PACK))
+        load_scale_rows(nc.sync, w1s_raw, w1_scales)
+        d_rows = d_scales[0].rearrange("(r e) n -> e r n", e=2)
+        for e in range(2):
+            nc.sync.dma_start(ds_tab[e:P:16, :].bitcast(I32), d_rows[e].bitcast(I32))
+        n2_l = load_list("n2_l", n2)
+        n1_l = load_list("n1_l", n1)
+        n3_l = load_list("n3_l", n3)
+        n4_l = load_list("n4_l", n4)
+        n5_l = load_list("n5_l", n5)
+
+        def pick_words(name, table, lst):
+            words = sb(name, [P, S], I32)
+            nc.vector.tensor_copy(words[:].bitcast(U32), table[:].bitcast(U32).indirect(lst[:]))
+            return words
+
+        def pick_scales(name, table, lst):
+            scales = sb(name, [P, S], U8)
+            nc.vector.tensor_copy(scales[:], table[:].indirect(lst[:]))
+            return scales
+
+        def deal(name, src, dtype, per_column):
+            dst = sb(name, [P, H * per_column], dtype)
+            nc.vector.tensor_copy(
+                dst[:].rearrange("p (t m b) -> p t m b", t=PACK, b=per_column),
+                src[:].rearrange("p (m t b) -> p t m b", t=PACK, b=per_column),
+            )
+            return dst
+
+        def first_layer(bank0, w_words, w_scales, xw, xs):
+            banks = []
+            for t in range(PACK):
+                bank = psum.tile([P, S], F32, name="bank", tag="bank%d" % (bank0 + t))
+                nc.tensor.matmul_mx(
+                    bank[:],
+                    lhsT=w_words[:, 2 * P * t : 2 * P * (t + 1)].bitcast(FP4X4),
+                    lhsT_scale=w_scales[:, P * t : P * (t + 1)],
+                    rhs=xw[:].bitcast(FP8X4),
+                    rhs_scale=xs[:],
+                    start=True,
+                    stop=True,
+                )
+                banks.append(bank)
+            return banks
+
+        w2w = deal("w2w", w2w_raw, U8, 2)
+        w1w = deal("w1w", w1w_raw, U8, 2)
+        x2w = pick_words("x2w", xw_tab, two_l)
+        x1w = pick_words("x1w", xw_tab, offs_l)
+        x2s = pick_scales("x2s", xs_tab, two_l)
+        w2s = deal("w2s", w2s_raw, U8, 1)
+        d_banks = first_layer(0, w2w, w2s, x2w, x2s)
+        x1s = pick_scales("x1s", xs_tab, offs_l)
+        w1s = deal("w1s", w1s_raw, U8, 1)
+        y_banks = first_layer(PACK, w1w, w1s, x1w, x1s)
+
+        ds_pick = pick_scales("ds_pick", ds_tab, k1_l)
+        dw_pick = pick_words("dw_pick", dw_tab, k1_l)
+        dw = deal("dw", dw_pick, I32, 1)
+        ds = deal("ds", ds_pick, U8, 1)
+        for e in range(2):
+            nc.sync.dma_start(ds[2 + e : P : 32, :].bitcast(I32), ds[16 + e : P : 32, :].bitcast(I32))
+
+        tanh_d, d_g, y_g = [], [], []
+        for t in range(PACK):
+            tanh_d.append(sb("tanh_d%d" % t, [P, S], F32))
+            nc.scalar.activation(tanh_d[t][:], d_banks[t][:], ACT.Tanh)
+            d_g.append(sb("d_g%d" % t, [P, S], F32))
+            nc.scalar.activation(d_g[t][:], d_banks[t][:], ACT.Copy, scale=gain[:, t : t + 1])
+        for t in range(PACK):
+            y_g.append(sb("y_g%d" % t, [P, S], F32))
+            nc.scalar.activation(y_g[t][:], y_banks[t][:], ACT.Copy, scale=gain[:, t : t + 1])
+
+        h_banks = [psum.tile([P, S], F32, name="bank", tag="bank%d" % t) for t in range(PACK)]
+        ex = [sb("ex%d" % t, [P, S], F32) for t in range(PACK)]
+        half_h = [sb("half_h%d" % t, [P, S], F32) for t in range(PACK)]
+        ex_own = {}
+        for h in range(2):
+            cols = slice(h * HALF, (h + 1) * HALF)
+            prod = [sb("prod%d_%d" % (h, t), [P, HALF], F32) for t in range(PACK)]
+            z = sb("z%d" % h, [P, PACK, HALF], F32)
+            for t in range(PACK):
+                nc.vector.tensor_tensor(prod[t][:], d_g[t][:].indirect(half_of(n2_l, h)), tanh_d[t][:, cols], ALU.mult)
+            for t in range(PACK):
+                nc.vector.tensor_tensor(z[:, t, :], y_g[t][:].indirect(half_of(n1_l, h)), prod[t][:], ALU.subtract)
+            z_bf = sb("z_bf%d" % h, [P, HALF, PACK], BF16)
+            if h == 0:
+                nc.scalar.copy(z_bf[:], z[:].rearrange("p t j -> p j t"))
+            else:
+                nc.vector.tensor_copy(z_bf[:], z[:].rearrange("p t j -> p j t"))
+            z_words = sb("z_words%d" % h, [P, HALF], I32)
+            nc.vector.quantize_mx(z_words[:].bitcast(FP8X4), z_scales[h][:], z_bf[:].rearrange("p j t -> p (j t)"))
+            for t in range(PACK):
+                nc.tensor.matmul_mx(
+                    h_banks[t][:, cols],
+                    lhsT=dw[:, P * t : P * (t + 1)].bitcast(FP8X4),
+                    lhsT_scale=ds[:, P * t : P * (t + 1)],
+                    rhs=z_words[:].bitcast(FP8X4),
+                    rhs_scale=z_scales[h][:],
+                    start=True,
+                    stop=True,
+                )
+            for t in range(PACK):
+                nc.scalar.activation(ex[t][:, cols], h_banks[t][:, cols], ACT.Exp, scale=0.03125)
+                ex_own[h, t] = sb("ex_own%d_%d" % (h, t), [P, HALF], F32)
+                nc.sync.dma_start(ex_own[h, t][:], ex[t][:, cols])
+            if h == 0:
+                for t in range(PACK):
+                    nc.scalar.activation(half_h[t][:, cols], h_banks[t][:, cols], ACT.Copy, scale=0.03125)
+
+        ex4 = {}
+        for h in range(2):
+            for t in range(PACK):
+                if h == 0:
+                    nc.scalar.activation(half_h[t][:, HALF:], h_banks[t][:, HALF:], ACT.Copy, scale=0.03125)
+                ex4[h, t] = sb("ex4_%d_%d" % (h, t), [P, HALF], F32)
+                nc.scalar.activation(ex4[h, t][:], half_h[t][:].indirect(half_of(n4_l, h)), ACT.Exp)
+
+        sums = {}
+        for h in range(2):
+            for t in range(PACK):
+                sums[h, t] = sb("sums%d_%d" % (h, t), [P, 2, HALF], F32)
+                nc.vector.tensor_tensor(sums[h, t][:, 0, :], ex[t][:].indirect(half_of(n3_l, h)), ex_own[h, t][:], ALU.add)
+            for t in range(PACK):
+                nc.vector.tensor_tensor(sums[h, t][:, 1, :], ex[t][:].indirect(half_of(n5_l, h)), ex4[h, t][:], ALU.add)
+
+        out_rows = out_0.rearrange("(p t) j -> p t j", t=PACK)
+        o_scales = sb("o_scales", [P, S], U8)
+        for h in range(2):
+            cols = slice(h * HALF, (h + 1) * HALF)
+            res = sb("res%d" % h, [P, PACK, HALF], F32)
+            for t in range(PACK):
+                logs = sb("logs%d_%d" % (h, t), [P, 2, HALF], F32)
+                nc.scalar.activation(logs[:], sums[h, t][:], ACT.Ln)
+                nc.vector.tensor_tensor(res[:, t, :], logs[:, 0, :], logs[:, 1, :], ALU.subtract)
+            nc.sync.dma_start(out_rows[:, :, cols], res[:])
+            o_bf = sb("o_bf%d" % h, [P, HALF, PACK], BF16)
+            nc.vector.tensor_copy(o_bf[:], res[:].rearrange("p t j -> p j t"))
+            o_words = sb("o_words%d" % h, [P, HALF], I32)
+            nc.vector.quantize_mx(o_words[:].bitcast(FP8X4), o_scales[:, cols], o_bf[:].rearrange("p j t -> p (j t)"))
+            nc.sync.dma_start(out_1[0, :, cols, :].rearrange("p c r -> p (c r)").bitcast(I32), o_words[:])
+        for q in range(4):
+            nc.scalar.dma_start(out_2[0, 4 * q : 4 * q + 4, :].bitcast(I32), o_scales[32 * q : 32 * q + 4, :].bitcast(I32))

@@ -18,6 +18,8 @@ PACK = 4
 K, T, S, H, G = 512, 1024, 512, 512, 2048
 HALF = S // 2
 LIST_COLS = S // 16
+Z_CHUNKS = ((0, 256), (256, 384), (384, 512))
+QUARTER = S // 4
 FLOPS = 3 * 2 * K * H * S
 
 
@@ -31,16 +33,19 @@ def tile_picked_twqsoftbodds_none_po_kernel(
         keep = ctx.enter_context(tc.tile_pool(name="keep", bufs=1))
         psum = ctx.enter_context(tc.psum_pool(name="psum", bufs=1))
 
-        def sb(name, shape, dtype):
-            return keep.tile(shape, dtype, name=name, align_bytes=64)
+        def sb(name, shape, dtype, tag=None):
+            return keep.tile(shape, dtype, name=name, tag=tag or name, align_bytes=64)
 
         def load_list(name, src):
             tile = lists.tile([P, LIST_COLS], U16, name=name)
             nc.sync.dma_start(tile[:], src)
             return tile
 
-        def half_of(lst, h):
-            return lst[:, h * (LIST_COLS // 2) : (h + 1) * (LIST_COLS // 2)]
+        def part(lst, c0, c1):
+            return lst[:, c0 // 16 : c1 // 16]
+
+        def weave(engine_copy, dst, src):
+            engine_copy(dst[:].rearrange("p (c i) t -> p c t i", i=4), src[:].rearrange("p t (c i) -> p c t i", i=4))
 
         def load_scale_rows(queue, dst, src):
             for q in range(4):
@@ -54,13 +59,12 @@ def tile_picked_twqsoftbodds_none_po_kernel(
         nc.vector.memset(w2s_raw[:].bitcast(I32), 0)
         nc.gpsimd.memset(w1s_raw[:].bitcast(I32), 0)
         nc.gpsimd.memset(ds_tab[:].bitcast(I32), 0)
-        z_scales = [sb("z_scales%d" % h, [P, HALF], U8) for h in range(2)]
-        for h in range(2):
-            nc.gpsimd.memset(z_scales[h][:].bitcast(I32), 0)
+        z_scales = sb("z_scales", [P, S], U8)
+        nc.gpsimd.memset(z_scales[:].bitcast(I32), 0)
 
-        w2w_raw = sb("w2w_raw", [P, 2 * H], U8)
+        w2w_raw = sb("w2w_raw", [P, H], U16)
         nc.sync.dma_start(w2w_raw[:].bitcast(I32), w2_words[0].bitcast(I32))
-        w1w_raw = sb("w1w_raw", [P, 2 * H], U8)
+        w1w_raw = sb("w1w_raw", [P, H], U16)
         nc.scalar.dma_start(w1w_raw[:].bitcast(I32), w1_words[0].bitcast(I32))
         two_l = load_list("two_l", two)
         xw_tab = sb("xw_tab", [P, T], I32)
@@ -68,15 +72,15 @@ def tile_picked_twqsoftbodds_none_po_kernel(
         load_scale_rows(nc.scalar, xs_tab, x_scales)
         offs_l = load_list("offs_l", offs)
         load_scale_rows(nc.scalar, w2s_raw, w2_scales)
-        k1_l = load_list("k1_l", k1)
-        dw_tab = sb("dw_tab", [P, G], I32)
-        nc.sync.dma_start(dw_tab[:], d_words[0].rearrange("p n r -> p (n r)").bitcast(I32))
         gain = sb("gain", [P, PACK], F32)
         nc.sync.dma_start(gain[:], gs.rearrange("(p t) o -> p (t o)", t=PACK))
+        k1_l = load_list("k1_l", k1)
         load_scale_rows(nc.sync, w1s_raw, w1_scales)
         d_rows = d_scales[0].rearrange("(r e) n -> e r n", e=2)
         for e in range(2):
             nc.sync.dma_start(ds_tab[e:P:16, :].bitcast(I32), d_rows[e].bitcast(I32))
+        dw_tab = sb("dw_tab", [P, G], I32)
+        nc.sync.dma_start(dw_tab[:], d_words[0].rearrange("p n r -> p (n r)").bitcast(I32))
         n2_l = load_list("n2_l", n2)
         n1_l = load_list("n1_l", n1)
         n3_l = load_list("n3_l", n3)
@@ -96,8 +100,8 @@ def tile_picked_twqsoftbodds_none_po_kernel(
         def deal(name, src, dtype, per_column):
             dst = sb(name, [P, H * per_column], dtype)
             nc.vector.tensor_copy(
-                dst[:].rearrange("p (t m b) -> p t m b", t=PACK, b=per_column),
-                src[:].rearrange("p (m t b) -> p t m b", t=PACK, b=per_column),
+                dst[:].rearrange("p (t m b) -> p m t b", t=PACK, b=per_column),
+                src[:].rearrange("p (m t b) -> p m t b", t=PACK, b=per_column),
             )
             return dst
 
@@ -107,7 +111,7 @@ def tile_picked_twqsoftbodds_none_po_kernel(
                 bank = psum.tile([P, S], F32, name="bank", tag="bank%d" % (bank0 + t))
                 nc.tensor.matmul_mx(
                     bank[:],
-                    lhsT=w_words[:, 2 * P * t : 2 * P * (t + 1)].bitcast(FP4X4),
+                    lhsT=w_words[:, P * t : P * (t + 1)].bitcast(FP4X4),
                     lhsT_scale=w_scales[:, P * t : P * (t + 1)],
                     rhs=xw[:].bitcast(FP8X4),
                     rhs_scale=xs[:],
@@ -117,8 +121,8 @@ def tile_picked_twqsoftbodds_none_po_kernel(
                 banks.append(bank)
             return banks
 
-        w2w = deal("w2w", w2w_raw, U8, 2)
-        w1w = deal("w1w", w1w_raw, U8, 2)
+        w2w = deal("w2w", w2w_raw, U16, 1)
+        w1w = deal("w1w", w1w_raw, U16, 1)
         x2w = pick_words("x2w", xw_tab, two_l)
         x1w = pick_words("x1w", xw_tab, offs_l)
         x2s = pick_scales("x2s", xs_tab, two_l)
@@ -130,8 +134,8 @@ def tile_picked_twqsoftbodds_none_po_kernel(
 
         ds_pick = pick_scales("ds_pick", ds_tab, k1_l)
         dw_pick = pick_words("dw_pick", dw_tab, k1_l)
-        dw = deal("dw", dw_pick, I32, 1)
         ds = deal("ds", ds_pick, U8, 1)
+        dw = deal("dw", dw_pick, I32, 1)
         for e in range(2):
             nc.sync.dma_start(ds[2 + e : P : 32, :].bitcast(I32), ds[16 + e : P : 32, :].bitcast(I32))
 
@@ -145,73 +149,103 @@ def tile_picked_twqsoftbodds_none_po_kernel(
             y_g.append(sb("y_g%d" % t, [P, S], F32))
             nc.scalar.activation(y_g[t][:], y_banks[t][:], ACT.Copy, scale=gain[:, t : t + 1])
 
-        h_banks = [psum.tile([P, S], F32, name="bank", tag="bank%d" % t) for t in range(PACK)]
-        ex = [sb("ex%d" % t, [P, S], F32) for t in range(PACK)]
+        ex_win = [sb("ex_win%d" % t, [P, 2 * S], F32) for t in range(PACK)]
         half_h = [sb("half_h%d" % t, [P, S], F32) for t in range(PACK)]
-        ex_own = {}
-        for h in range(2):
-            cols = slice(h * HALF, (h + 1) * HALF)
-            prod = [sb("prod%d_%d" % (h, t), [P, HALF], F32) for t in range(PACK)]
-            z = sb("z%d" % h, [P, PACK, HALF], F32)
+        ex_own = [sb("ex_own%d" % t, [P, S], F32) for t in range(PACK)]
+        late_copies = []
+        for c, (c0, c1) in enumerate(Z_CHUNKS):
+            last = c == len(Z_CHUNKS) - 1
+            width = c1 - c0
+            if c0 % HALF == 0:
+                for t in range(PACK):
+                    nc.vector.tensor_tensor(
+                        ex_win[t][:, S + c0 : S + c0 + HALF],
+                        d_g[t][:].indirect(part(n2_l, c0, c0 + HALF)),
+                        tanh_d[t][:, c0 : c0 + HALF],
+                        ALU.mult,
+                    )
+            z = sb("z%d" % c, [P, PACK, width], F32)
             for t in range(PACK):
-                nc.vector.tensor_tensor(prod[t][:], d_g[t][:].indirect(half_of(n2_l, h)), tanh_d[t][:, cols], ALU.mult)
+                nc.vector.tensor_tensor(
+                    z[:, t, :], y_g[t][:].indirect(part(n1_l, c0, c1)), ex_win[t][:, S + c0 : S + c1], ALU.subtract
+                )
+            z_bf = sb("z_bf%d" % c, [P, width, PACK], BF16)
+            weave(nc.scalar.copy if c < 2 else nc.vector.tensor_copy, z_bf, z)
+            z_words = sb("z_words%d" % c, [P, width], I32)
+            nc.vector.quantize_mx(z_words[:].bitcast(FP8X4), z_scales[:, c0:c1], z_bf[:].rearrange("p j t -> p (j t)"))
+            h_banks = []
             for t in range(PACK):
-                nc.vector.tensor_tensor(z[:, t, :], y_g[t][:].indirect(half_of(n1_l, h)), prod[t][:], ALU.subtract)
-            z_bf = sb("z_bf%d" % h, [P, HALF, PACK], BF16)
-            if h == 0:
-                nc.scalar.copy(z_bf[:], z[:].rearrange("p t j -> p j t"))
-            else:
-                nc.vector.tensor_copy(z_bf[:], z[:].rearrange("p t j -> p j t"))
-            z_words = sb("z_words%d" % h, [P, HALF], I32)
-            nc.vector.quantize_mx(z_words[:].bitcast(FP8X4), z_scales[h][:], z_bf[:].rearrange("p j t -> p (j t)"))
-            for t in range(PACK):
+                bank = psum.tile([P, S], F32, name="bank", tag="bank%d" % (PACK * (c % 2) + t))
                 nc.tensor.matmul_mx(
-                    h_banks[t][:, cols],
+                    bank[:, :width],
                     lhsT=dw[:, P * t : P * (t + 1)].bitcast(FP8X4),
                     lhsT_scale=ds[:, P * t : P * (t + 1)],
                     rhs=z_words[:].bitcast(FP8X4),
-                    rhs_scale=z_scales[h][:],
+                    rhs_scale=z_scales[:, c0:c1],
                     start=True,
                     stop=True,
                 )
+                h_banks.append(bank)
             for t in range(PACK):
-                nc.scalar.activation(ex[t][:, cols], h_banks[t][:, cols], ACT.Exp, scale=0.03125)
-                ex_own[h, t] = sb("ex_own%d_%d" % (h, t), [P, HALF], F32)
-                nc.sync.dma_start(ex_own[h, t][:], ex[t][:, cols])
-            if h == 0:
-                for t in range(PACK):
-                    nc.scalar.activation(half_h[t][:, cols], h_banks[t][:, cols], ACT.Copy, scale=0.03125)
+                nc.scalar.activation(ex_win[t][:, c0:c1], h_banks[t][:, :width], ACT.Exp, scale=0.03125)
+                nc.sync.dma_start(ex_own[t][:, c0:c1], ex_win[t][:, c0:c1])
+            for t in range(PACK):
+                if last:
+                    late_copies.append((half_h[t][:, c0:c1], h_banks[t][:, :width]))
+                else:
+                    nc.scalar.activation(half_h[t][:, c0:c1], h_banks[t][:, :width], ACT.Copy, scale=0.03125)
 
-        ex4 = {}
-        for h in range(2):
-            for t in range(PACK):
-                if h == 0:
-                    nc.scalar.activation(half_h[t][:, HALF:], h_banks[t][:, HALF:], ACT.Copy, scale=0.03125)
-                ex4[h, t] = sb("ex4_%d_%d" % (h, t), [P, HALF], F32)
-                nc.scalar.activation(ex4[h, t][:], half_h[t][:].indirect(half_of(n4_l, h)), ACT.Exp)
+        ex4 = [sb("ex4_%d" % t, [P, S], F32) for t in range(PACK)]
+        for t in range(PACK):
+            nc.scalar.activation(late_copies[t][0], late_copies[t][1], ACT.Copy, scale=0.03125)
+            for c0 in (0, HALF):
+                nc.scalar.activation(ex4[t][:, c0 : c0 + HALF], half_h[t][:].indirect(part(n4_l, c0, c0 + HALF)), ACT.Exp)
 
-        sums = {}
-        for h in range(2):
-            for t in range(PACK):
-                sums[h, t] = sb("sums%d_%d" % (h, t), [P, 2, HALF], F32)
-                nc.vector.tensor_tensor(sums[h, t][:, 0, :], ex[t][:].indirect(half_of(n3_l, h)), ex_own[h, t][:], ALU.add)
-            for t in range(PACK):
-                nc.vector.tensor_tensor(sums[h, t][:, 1, :], ex[t][:].indirect(half_of(n5_l, h)), ex4[h, t][:], ALU.add)
+        num = sb("num", [P, PACK, S], F32)
+        den = sb("den", [P, PACK, S], F32)
+
+        def numerator(t, c0):
+            nc.vector.tensor_tensor(
+                num[:, t, c0 : c0 + HALF],
+                ex_win[t][:].indirect(part(n3_l, c0, c0 + HALF)),
+                ex_own[t][:, c0 : c0 + HALF],
+                ALU.add,
+            )
+
+        for t in range(PACK):
+            numerator(t, 0)
+        for t in range(PACK):
+            nc.vector.tensor_tensor(den[:, t, :], ex_win[t][:].indirect(n5_l[:]), ex4[t][:], ALU.add)
+            numerator(t, HALF)
 
         out_rows = out_0.rearrange("(p t) j -> p t j", t=PACK)
         o_scales = sb("o_scales", [P, S], U8)
         for h in range(2):
-            cols = slice(h * HALF, (h + 1) * HALF)
-            res = sb("res%d" % h, [P, PACK, HALF], F32)
-            for t in range(PACK):
-                logs = sb("logs%d_%d" % (h, t), [P, 2, HALF], F32)
-                nc.scalar.activation(logs[:], sums[h, t][:], ACT.Ln)
-                nc.vector.tensor_tensor(res[:, t, :], logs[:, 0, :], logs[:, 1, :], ALU.subtract)
-            nc.sync.dma_start(out_rows[:, :, cols], res[:])
-            o_bf = sb("o_bf%d" % h, [P, HALF, PACK], BF16)
-            nc.vector.tensor_copy(o_bf[:], res[:].rearrange("p t j -> p j t"))
+            c0 = h * HALF
+            log_num = sb("log_num%d" % h, [P, PACK, HALF], F32, "half_h%d" % (PACK - 1 - h))
+            nc.scalar.activation(log_num[:], num[:, :, c0 : c0 + HALF], ACT.Ln)
+            log_den = sb("log_den%d" % h, [P, PACK, HALF], F32)
+            pieces = ((0, HALF),) if h == 0 else ((0, QUARTER), (QUARTER, HALF))
+            for a, b in pieces:
+                nc.scalar.activation(log_den[:, :, a:b], den[:, :, c0 + a : c0 + b], ACT.Ln)
+            starts = (0, QUARTER)
+            res = [sb("res%d_%d" % (h, a), [P, PACK, QUARTER], F32) for a in starts]
+            o_bf = [sb("o_bf%d_%d" % (h, a), [P, QUARTER, PACK], BF16) for a in starts]
             o_words = sb("o_words%d" % h, [P, HALF], I32)
-            nc.vector.quantize_mx(o_words[:].bitcast(FP8X4), o_scales[:, cols], o_bf[:].rearrange("p j t -> p (j t)"))
-            nc.sync.dma_start(out_1[0, :, cols, :].rearrange("p c r -> p (c r)").bitcast(I32), o_words[:])
+            for i, a in enumerate(starts):
+                nc.vector.tensor_tensor(
+                    res[i][:], log_num[:, :, a : a + QUARTER], log_den[:, :, a : a + QUARTER], ALU.subtract
+                )
+                nc.sync.dma_start(out_rows[:, :, c0 + a : c0 + a + QUARTER], res[i][:])
+            for i in range(2):
+                weave(nc.vector.tensor_copy, o_bf[i], res[i])
+            for i, a in enumerate(starts):
+                nc.vector.quantize_mx(
+                    o_words[:, a : a + QUARTER].bitcast(FP8X4),
+                    o_scales[:, c0 + a : c0 + a + QUARTER],
+                    o_bf[i][:].rearrange("p j t -> p (j t)"),
+                )
+            nc.sync.dma_start(out_1[0, :, c0 : c0 + HALF, :].rearrange("p c r -> p (c r)").bitcast(I32), o_words[:])
         for q in range(4):
-            nc.scalar.dma_start(out_2[0, 4 * q : 4 * q + 4, :].bitcast(I32), o_scales[32 * q : 32 * q + 4, :].bitcast(I32))
+            queue = nc.sync if q == 0 else nc.scalar
+            queue.dma_start(out_2[0, 4 * q : 4 * q + 4, :].bitcast(I32), o_scales[32 * q : 32 * q + 4, :].bitcast(I32))

@@ -55,22 +55,22 @@ def tile_picked_twqsoftbodds_none_po_kernel(
         w2s_raw = sb("w2s_raw", [P, H], U8)
         w1s_raw = sb("w1s_raw", [P, H], U8)
         ds_tab = sb("ds_tab", [P, G], U8)
-        nc.vector.memset(xs_tab[:].bitcast(I32), 0)
-        nc.vector.memset(w2s_raw[:].bitcast(I32), 0)
+        nc.gpsimd.memset(xs_tab[:].bitcast(I32), 0)
+        nc.gpsimd.memset(w2s_raw[:].bitcast(I32), 0)
         nc.gpsimd.memset(w1s_raw[:].bitcast(I32), 0)
         nc.gpsimd.memset(ds_tab[:].bitcast(I32), 0)
         z_scales = sb("z_scales", [P, S], U8)
         nc.gpsimd.memset(z_scales[:].bitcast(I32), 0)
 
+        two_l = load_list("two_l", two)
+        load_scale_rows(nc.scalar, xs_tab, x_scales)
+        offs_l = load_list("offs_l", offs)
         w2w_raw = sb("w2w_raw", [P, H], U16)
         nc.sync.dma_start(w2w_raw[:].bitcast(I32), w2_words[0].bitcast(I32))
         w1w_raw = sb("w1w_raw", [P, H], U16)
-        nc.scalar.dma_start(w1w_raw[:].bitcast(I32), w1_words[0].bitcast(I32))
-        two_l = load_list("two_l", two)
+        nc.sync.dma_start(w1w_raw[:].bitcast(I32), w1_words[0].bitcast(I32))
         xw_tab = sb("xw_tab", [P, T], I32)
         nc.sync.dma_start(xw_tab[:], x_words[0].rearrange("p n r -> p (n r)").bitcast(I32))
-        load_scale_rows(nc.scalar, xs_tab, x_scales)
-        offs_l = load_list("offs_l", offs)
         load_scale_rows(nc.scalar, w2s_raw, w2_scales)
         gain = sb("gain", [P, PACK], F32)
         nc.sync.dma_start(gain[:], gs.rearrange("(p t) o -> p (t o)", t=PACK))
@@ -123,12 +123,12 @@ def tile_picked_twqsoftbodds_none_po_kernel(
 
         w2w = deal("w2w", w2w_raw, U16, 1)
         w1w = deal("w1w", w1w_raw, U16, 1)
-        x2w = pick_words("x2w", xw_tab, two_l)
-        x1w = pick_words("x1w", xw_tab, offs_l)
         x2s = pick_scales("x2s", xs_tab, two_l)
+        x1s = pick_scales("x1s", xs_tab, offs_l)
+        x2w = pick_words("x2w", xw_tab, two_l)
         w2s = deal("w2s", w2s_raw, U8, 1)
         d_banks = first_layer(0, w2w, w2s, x2w, x2s)
-        x1s = pick_scales("x1s", xs_tab, offs_l)
+        x1w = pick_words("x1w", xw_tab, offs_l)
         w1s = deal("w1s", w1s_raw, U8, 1)
         y_banks = first_layer(PACK, w1w, w1s, x1w, x1s)
 
@@ -139,43 +139,47 @@ def tile_picked_twqsoftbodds_none_po_kernel(
         for e in range(2):
             nc.sync.dma_start(ds[2 + e : P : 32, :].bitcast(I32), ds[16 + e : P : 32, :].bitcast(I32))
 
-        tanh_d, d_g, y_g = [], [], []
+        ex_win = [sb("ex_win%d" % t, [P, 2 * S], F32) for t in range(PACK)]
+        d_g, y_g = [], []
         for t in range(PACK):
-            tanh_d.append(sb("tanh_d%d" % t, [P, S], F32))
-            nc.scalar.activation(tanh_d[t][:], d_banks[t][:], ACT.Tanh)
+            nc.scalar.activation(ex_win[t][:, S : S + HALF], d_banks[t][:, :HALF], ACT.Tanh)
             d_g.append(sb("d_g%d" % t, [P, S], F32))
             nc.scalar.activation(d_g[t][:], d_banks[t][:], ACT.Copy, scale=gain[:, t : t + 1])
         for t in range(PACK):
             y_g.append(sb("y_g%d" % t, [P, S], F32))
             nc.scalar.activation(y_g[t][:], y_banks[t][:], ACT.Copy, scale=gain[:, t : t + 1])
+        for t in range(PACK):
+            nc.scalar.activation(ex_win[t][:, S + HALF :], d_banks[t][:, HALF:], ACT.Tanh)
 
-        ex_win = [sb("ex_win%d" % t, [P, 2 * S], F32) for t in range(PACK)]
         half_h = [sb("half_h%d" % t, [P, S], F32) for t in range(PACK)]
         ex_own = [sb("ex_own%d" % t, [P, S], F32) for t in range(PACK)]
-        late_copies = []
+        late_copies = [[] for t in range(PACK)]
         for c, (c0, c1) in enumerate(Z_CHUNKS):
-            last = c == len(Z_CHUNKS) - 1
             width = c1 - c0
             if c0 % HALF == 0:
+                half0 = c0
+                prod = [sb("prod%d_%d" % (c0, t), [P, HALF], F32)[:] for t in range(PACK - 2 * (c > 0))]
+                if c > 0:
+                    prod.extend([z[:, 2, :], z[:, 3, :]])
                 for t in range(PACK):
                     nc.vector.tensor_tensor(
-                        ex_win[t][:, S + c0 : S + c0 + HALF],
+                        prod[t],
                         d_g[t][:].indirect(part(n2_l, c0, c0 + HALF)),
-                        tanh_d[t][:, c0 : c0 + HALF],
+                        ex_win[t][:, S + c0 : S + c0 + HALF],
                         ALU.mult,
                     )
             z = sb("z%d" % c, [P, PACK, width], F32)
             for t in range(PACK):
                 nc.vector.tensor_tensor(
-                    z[:, t, :], y_g[t][:].indirect(part(n1_l, c0, c1)), ex_win[t][:, S + c0 : S + c1], ALU.subtract
+                    z[:, t, :], y_g[t][:].indirect(part(n1_l, c0, c1)), prod[t][:, c0 - half0 : c1 - half0], ALU.subtract
                 )
-            z_bf = sb("z_bf%d" % c, [P, width, PACK], BF16)
+            z_bf = sb("z_bf%d" % c, [P, width, PACK], BF16, "z1" if c == 2 else None)
             weave(nc.scalar.copy if c < 2 else nc.vector.tensor_copy, z_bf, z)
             z_words = sb("z_words%d" % c, [P, width], I32)
             nc.vector.quantize_mx(z_words[:].bitcast(FP8X4), z_scales[:, c0:c1], z_bf[:].rearrange("p j t -> p (j t)"))
             h_banks = []
             for t in range(PACK):
-                bank = psum.tile([P, S], F32, name="bank", tag="bank%d" % (PACK * (c % 2) + t))
+                bank = psum.tile([P, S], F32, name="bank", tag="bank%d" % (PACK * ((c + 1) % 2) + t))
                 nc.tensor.matmul_mx(
                     bank[:, :width],
                     lhsT=dw[:, P * t : P * (t + 1)].bitcast(FP8X4),
@@ -190,14 +194,15 @@ def tile_picked_twqsoftbodds_none_po_kernel(
                 nc.scalar.activation(ex_win[t][:, c0:c1], h_banks[t][:, :width], ACT.Exp, scale=0.03125)
                 nc.sync.dma_start(ex_own[t][:, c0:c1], ex_win[t][:, c0:c1])
             for t in range(PACK):
-                if last:
-                    late_copies.append((half_h[t][:, c0:c1], h_banks[t][:, :width]))
+                if c > 0:
+                    late_copies[t].append((half_h[t][:, c0:c1], h_banks[t][:, :width]))
                 else:
                     nc.scalar.activation(half_h[t][:, c0:c1], h_banks[t][:, :width], ACT.Copy, scale=0.03125)
 
         ex4 = [sb("ex4_%d" % t, [P, S], F32) for t in range(PACK)]
         for t in range(PACK):
-            nc.scalar.activation(late_copies[t][0], late_copies[t][1], ACT.Copy, scale=0.03125)
+            for dst, src in late_copies[t]:
+                nc.scalar.activation(dst, src, ACT.Copy, scale=0.03125)
             for c0 in (0, HALF):
                 nc.scalar.activation(ex4[t][:, c0 : c0 + HALF], half_h[t][:].indirect(part(n4_l, c0, c0 + HALF)), ACT.Exp)
 
@@ -238,7 +243,7 @@ def tile_picked_twqsoftbodds_none_po_kernel(
                 )
                 nc.sync.dma_start(out_rows[:, :, c0 + a : c0 + a + QUARTER], res[i][:])
             for i in range(2):
-                weave(nc.vector.tensor_copy, o_bf[i], res[i])
+                weave(nc.scalar.copy if (h, i) == (1, 0) else nc.vector.tensor_copy, o_bf[i], res[i])
             for i, a in enumerate(starts):
                 nc.vector.quantize_mx(
                     o_words[:, a : a + QUARTER].bitcast(FP8X4),

@@ -45,7 +45,7 @@ def tile_picked_twqsoftbodds_none_po_kernel(
             return lst[:, c0 // 16 : c1 // 16]
 
         def weave(engine_copy, dst, src):
-            engine_copy(dst[:].rearrange("p (c i) t -> p c t i", i=4), src[:].rearrange("p t (c i) -> p c t i", i=4))
+            engine_copy(dst[:].rearrange("p (c i) t -> p c t i", i=4), src.rearrange("p t (c i) -> p c t i", i=4))
 
         def load_scale_rows(queue, dst, src):
             for q in range(4):
@@ -79,7 +79,7 @@ def tile_picked_twqsoftbodds_none_po_kernel(
         d_rows = d_scales[0].rearrange("(r e) n -> e r n", e=2)
         for e in range(2):
             nc.sync.dma_start(ds_tab[e:P:16, :].bitcast(I32), d_rows[e].bitcast(I32))
-        dw_tab = sb("dw_tab", [P, G], I32)
+        dw_tab = sb("dw_tab", [P, G], I32, "w1w_raw")
         nc.sync.dma_start(dw_tab[:], d_words[0].rearrange("p n r -> p (n r)").bitcast(I32))
         n2_l = load_list("n2_l", n2)
         n1_l = load_list("n1_l", n1)
@@ -153,6 +153,8 @@ def tile_picked_twqsoftbodds_none_po_kernel(
 
         half_h = [sb("half_h%d" % t, [P, S], F32) for t in range(PACK)]
         ex_own = [sb("ex_own%d" % t, [P, S], F32) for t in range(PACK)]
+        held_copies = []
+        gap_copies = []
         late_copies = [[] for t in range(PACK)]
         for c, (c0, c1) in enumerate(Z_CHUNKS):
             width = c1 - c0
@@ -168,15 +170,22 @@ def tile_picked_twqsoftbodds_none_po_kernel(
                         ex_win[t][:, S + c0 : S + c0 + HALF],
                         ALU.mult,
                     )
-            z = sb("z%d" % c, [P, PACK, width], F32)
-            for t in range(PACK):
+            if c < 2:
+                z_tile = sb("z%d" % c, [P, PACK + 3 * c, width], F32)
+            z = z_tile[:, 3:, :] if c == 2 else z_tile[:, :PACK, :]
+            for t in (1, 2, 3, 0) if c == 2 else range(PACK):
                 nc.vector.tensor_tensor(
                     z[:, t, :], y_g[t][:].indirect(part(n1_l, c0, c1)), prod[t][:, c0 - half0 : c1 - half0], ALU.subtract
                 )
-            z_bf = sb("z_bf%d" % c, [P, width, PACK], BF16, "z1" if c == 2 else None)
+            z_bf = sb("z_bf%d" % c, [P, width, PACK], BF16)
             weave(nc.scalar.copy if c < 2 else nc.vector.tensor_copy, z_bf, z)
+            for dst, src in held_copies:
+                nc.scalar.activation(dst, src, ACT.Copy, scale=0.03125)
+            held_copies = []
             z_words = sb("z_words%d" % c, [P, width], I32)
             nc.vector.quantize_mx(z_words[:].bitcast(FP8X4), z_scales[:, c0:c1], z_bf[:].rearrange("p j t -> p (j t)"))
+            for dst, src in gap_copies:
+                nc.vector.tensor_scalar_mul(dst, src, 0.03125)
             h_banks = []
             for t in range(PACK):
                 bank = psum.tile([P, S], F32, name="bank", tag="bank%d" % (PACK * ((c + 1) % 2) + t))
@@ -194,8 +203,12 @@ def tile_picked_twqsoftbodds_none_po_kernel(
                 nc.scalar.activation(ex_win[t][:, c0:c1], h_banks[t][:, :width], ACT.Exp, scale=0.03125)
                 nc.sync.dma_start(ex_own[t][:, c0:c1], ex_win[t][:, c0:c1])
             for t in range(PACK):
-                if c > 0:
+                if c == 2:
                     late_copies[t].append((half_h[t][:, c0:c1], h_banks[t][:, :width]))
+                elif c == 1:
+                    gap_copies.append((half_h[t][:, c0:c1], h_banks[t][:, :width]))
+                elif t > 0:
+                    held_copies.append((half_h[t][:, c0:c1], h_banks[t][:, :width]))
                 else:
                     nc.scalar.activation(half_h[t][:, c0:c1], h_banks[t][:, :width], ACT.Copy, scale=0.03125)
 
@@ -206,12 +219,12 @@ def tile_picked_twqsoftbodds_none_po_kernel(
             for c0 in (0, HALF):
                 nc.scalar.activation(ex4[t][:, c0 : c0 + HALF], half_h[t][:].indirect(part(n4_l, c0, c0 + HALF)), ACT.Exp)
 
-        num = sb("num", [P, PACK, S], F32)
+        num = [sb("num0", [P, PACK, HALF], F32), sb("num1", [P, PACK, HALF], F32, "half_h2")]
         den = sb("den", [P, PACK, S], F32)
 
         def numerator(t, c0):
             nc.vector.tensor_tensor(
-                num[:, t, c0 : c0 + HALF],
+                num[c0 // HALF][:, t, :],
                 ex_win[t][:].indirect(part(n3_l, c0, c0 + HALF)),
                 ex_own[t][:, c0 : c0 + HALF],
                 ALU.add,
@@ -221,36 +234,52 @@ def tile_picked_twqsoftbodds_none_po_kernel(
             numerator(t, 0)
         for t in range(PACK):
             nc.vector.tensor_tensor(den[:, t, :], ex_win[t][:].indirect(n5_l[:]), ex4[t][:], ALU.add)
+        for t in range(PACK):
             numerator(t, HALF)
 
         out_rows = out_0.rearrange("(p t) j -> p t j", t=PACK)
         o_scales = sb("o_scales", [P, S], U8)
+        log_num = [sb("log_num0", [P, PACK, HALF], F32, "half_h3"), sb("log_num1", [P, PACK, HALF], F32)]
+        log_den = [sb("log_den%d" % h, [P, PACK, HALF], F32) for h in range(2)]
+        nc.scalar.activation(log_num[0][:], num[0][:], ACT.Ln)
         for h in range(2):
-            c0 = h * HALF
-            log_num = sb("log_num%d" % h, [P, PACK, HALF], F32, "half_h%d" % (PACK - 1 - h))
-            nc.scalar.activation(log_num[:], num[:, :, c0 : c0 + HALF], ACT.Ln)
-            log_den = sb("log_den%d" % h, [P, PACK, HALF], F32)
-            pieces = ((0, HALF),) if h == 0 else ((0, QUARTER), (QUARTER, HALF))
-            for a, b in pieces:
-                nc.scalar.activation(log_den[:, :, a:b], den[:, :, c0 + a : c0 + b], ACT.Ln)
-            starts = (0, QUARTER)
-            res = [sb("res%d_%d" % (h, a), [P, PACK, QUARTER], F32) for a in starts]
-            o_bf = [sb("o_bf%d_%d" % (h, a), [P, QUARTER, PACK], BF16) for a in starts]
-            o_words = sb("o_words%d" % h, [P, HALF], I32)
-            for i, a in enumerate(starts):
-                nc.vector.tensor_tensor(
-                    res[i][:], log_num[:, :, a : a + QUARTER], log_den[:, :, a : a + QUARTER], ALU.subtract
-                )
-                nc.sync.dma_start(out_rows[:, :, c0 + a : c0 + a + QUARTER], res[i][:])
-            for i in range(2):
-                weave(nc.scalar.copy if (h, i) == (1, 0) else nc.vector.tensor_copy, o_bf[i], res[i])
-            for i, a in enumerate(starts):
-                nc.vector.quantize_mx(
-                    o_words[:, a : a + QUARTER].bitcast(FP8X4),
-                    o_scales[:, c0 + a : c0 + a + QUARTER],
-                    o_bf[i][:].rearrange("p j t -> p (j t)"),
-                )
-            nc.sync.dma_start(out_1[0, :, c0 : c0 + HALF, :].rearrange("p c r -> p (c r)").bitcast(I32), o_words[:])
+            nc.scalar.activation(log_den[h][:], den[:, :, h * HALF : (h + 1) * HALF], ACT.Ln)
+        for a in (0, QUARTER):
+            nc.scalar.activation(log_num[1][:, :, a : a + QUARTER], num[1][:, :, a : a + QUARTER], ACT.Ln)
+        res = [sb("res%d" % i, [P, PACK, QUARTER], F32) for i in range(4)]
+        o_bf = [sb("o_bf%d" % i, [P, QUARTER, PACK], BF16) for i in range(4)]
+        o_words = [sb("o_words%d" % h, [P, HALF], I32) for h in range(2)]
+
+        def difference(i):
+            h, a = i // 2, i % 2 * QUARTER
+            nc.vector.tensor_tensor(
+                res[i][:], log_num[h][:, :, a : a + QUARTER], log_den[h][:, :, a : a + QUARTER], ALU.subtract
+            )
+            nc.sync.dma_start(out_rows[:, :, i * QUARTER : (i + 1) * QUARTER], res[i][:])
+
+        def quantise(i):
+            h, a = i // 2, i % 2 * QUARTER
+            nc.vector.quantize_mx(
+                o_words[h][:, a : a + QUARTER].bitcast(FP8X4),
+                o_scales[:, i * QUARTER : (i + 1) * QUARTER],
+                o_bf[i][:].rearrange("p j t -> p (j t)"),
+            )
+            if a:
+                words_out = out_1[0, :, h * HALF : (h + 1) * HALF, :].rearrange("p c r -> p (c r)")
+                nc.sync.dma_start(words_out.bitcast(I32), o_words[h][:])
+
+        difference(0)
+        difference(1)
+        weave(nc.vector.tensor_copy, o_bf[0], res[0][:])
+        difference(2)
+        quantise(0)
+        difference(3)
+        weave(nc.scalar.copy, o_bf[1], res[1][:])
+        weave(nc.scalar.copy, o_bf[2], res[2][:])
+        quantise(1)
+        weave(nc.vector.tensor_copy, o_bf[3], res[3][:])
+        quantise(2)
+        quantise(3)
         for q in range(4):
             queue = nc.sync if q == 0 else nc.scalar
             queue.dma_start(out_2[0, 4 * q : 4 * q + 4, :].bitcast(I32), o_scales[32 * q : 32 * q + 4, :].bitcast(I32))

from contextlib import ExitStack

import concourse.mybir as mybir

F32 = mybir.dt.float32
BF16 = mybir.dt.bfloat16
I32 = mybir.dt.int32
U32 = mybir.dt.uint32
U16 = mybir.dt.uint16
U8 = mybir.dt.uint8
FP8X4 = mybir.dt.float8_e4m3fn_x4
FP4X4 = mybir.dt.float4_e2m1fn_x4
ACT = mybir.ActivationFunctionType
ALU = mybir.AluOpType

P = 128
PACK = 4
K, T, S, H, G = 512, 1024, 512, 512, 2048
HALF = S // 2
LIST_COLS = S // 16
Z_CHUNKS = ((0, 256), (256, 384), (384, 512))
QUARTER = S // 4
FLOPS = 3 * 2 * K * H * S


def tile_picked_twqsoftbodds_none_po_kernel(
    tc, x_words, x_scales, w1_words, w1_scales, w2_words, w2_scales, gs, d_words, d_scales,
    offs, two, n1, n2, k1, n3, n4, n5, out_0, out_1, out_2,
):
    nc = tc.nc
    with ExitStack() as ctx:
        lists = ctx.enter_context(tc.tile_pool(name="lists", bufs=1))
        keep = ctx.enter_context(tc.tile_pool(name="keep", bufs=1))
        psum = ctx.enter_context(tc.psum_pool(name="psum", bufs=1))

        def sb(name, shape, dtype, tag=None):
            return keep.tile(shape, dtype, name=name, tag=tag or name, align_bytes=64)

        def load_list(name, src):
            tile = lists.tile([P, LIST_COLS], U16, name=name)
            nc.sync.dma_start(tile[:], src)
            return tile

        def part(lst, c0, c1):
            return lst[:, c0 // 16 : c1 // 16]

        def weave(engine_copy, dst, src):
            engine_copy(dst[:].rearrange("p (c i) t -> p c t i", i=4), src.rearrange("p t (c i) -> p c t i", i=4))

        def load_scale_rows(queue, dst, src):
            for q in range(4):
                queue.dma_start(dst[32 * q : 32 * q + 4, :].bitcast(I32), src[0, 4 * q : 4 * q + 4, :].bitcast(I32))

        xs_tab = sb("xs_tab", [P, T], U8)
        w2s_raw = sb("w2s_raw", [P, H], U8)
        w1s_raw = sb("w1s_raw", [P, H], U8)
        ds_tab = sb("ds_tab", [P, G], U8)
        nc.gpsimd.memset(xs_tab[:].bitcast(I32), 0)
        nc.gpsimd.memset(w2s_raw[:].bitcast(I32), 0)
        nc.gpsimd.memset(w1s_raw[:].bitcast(I32), 0)
        nc.gpsimd.memset(ds_tab[:].bitcast(I32), 0)
        z_scales = sb("z_scales", [P, S], U8)
        nc.gpsimd.memset(z_scales[:].bitcast(I32), 0)

        two_l = load_list("two_l", two)
        load_scale_rows(nc.scalar, xs_tab, x_scales)
        offs_l = load_list("offs_l", offs)
        w2w_raw = sb("w2w_raw", [P, H], U16)
        nc.sync.dma_start(w2w_raw[:].bitcast(I32), w2_words[0].bitcast(I32))
        w1w_raw = sb("w1w_raw", [P, H], U16)
        nc.sync.dma_start(w1w_raw[:].bitcast(I32), w1_words[0].bitcast(I32))
        xw_tab = sb("xw_tab", [P, T], I32)
        nc.sync.dma_start(xw_tab[:], x_words[0].rearrange("p n r -> p (n r)").bitcast(I32))
        load_scale_rows(nc.scalar, w2s_raw, w2_scales)
        gain = sb("gain", [P, PACK], F32)
        nc.sync.dma_start(gain[:], gs.rearrange("(p t) o -> p (t o)", t=PACK))
        k1_l = load_list("k1_l", k1)
        load_scale_rows(nc.sync, w1s_raw, w1_scales)
        d_rows = d_scales[0].rearrange("(r e) n -> e r n", e=2)
        for e in range(2):
            nc.sync.dma_start(ds_tab[e:P:16, :].bitcast(I32), d_rows[e].bitcast(I32))
        dw_tab = sb("dw_tab", [P, G], I32, "w1w_raw")
        nc.sync.dma_start(dw_tab[:], d_words[0].rearrange("p n r -> p (n r)").bitcast(I32))
        n2_l = load_list("n2_l", n2)
        n1_l = load_list("n1_l", n1)
        n3_l = load_list("n3_l", n3)
        n4_l = load_list("n4_l", n4)
        n5_l = load_list("n5_l", n5)

        def pick_words(name, table, lst):
            words = sb(name, [P, S], I32)
            nc.vector.tensor_copy(words[:].bitcast(U32), table[:].bitcast(U32).indirect(lst[:]))
            return words

        def pick_scales(name, table, lst):
            scales = sb(name, [P, S], U8)
            nc.vector.tensor_copy(scales[:], table[:].indirect(lst[:]))
            return scales

        def deal(name, src, dtype, per_column):
            dst = sb(name, [P, H * per_column], dtype)
            nc.vector.tensor_copy(
                dst[:].rearrange("p (t m b) -> p m t b", t=PACK, b=per_column),
                src[:].rearrange("p (m t b) -> p m t b", t=PACK, b=per_column),
            )
            return dst

        def first_layer(bank0, w_words, w_scales, xw, xs):
            banks = []
            for t in range(PACK):
                bank = psum.tile([P, S], F32, name="bank", tag="bank%d" % (bank0 + t))
                nc.tensor.matmul_mx(
                    bank[:],
                    lhsT=w_words[:, P * t : P * (t + 1)].bitcast(FP4X4),
                    lhsT_scale=w_scales[:, P * t : P * (t + 1)],
                    rhs=xw[:].bitcast(FP8X4),
                    rhs_scale=xs[:],
                    start=True,
                    stop=True,
                )
                banks.append(bank)
            return banks

        w2w = deal("w2w", w2w_raw, U16, 1)
        w1w = deal("w1w", w1w_raw, U16, 1)
        x2s = pick_scales("x2s", xs_tab, two_l)
        x1s = pick_scales("x1s", xs_tab, offs_l)
        x2w = pick_words("x2w", xw_tab, two_l)
        w2s = deal("w2s", w2s_raw, U8, 1)
        d_banks = first_layer(0, w2w, w2s, x2w, x2s)
        x1w = pick_words("x1w", xw_tab, offs_l)
        w1s = deal("w1s", w1s_raw, U8, 1)
        y_banks = first_layer(PACK, w1w, w1s, x1w, x1s)

        ds_pick = pick_scales("ds_pick", ds_tab, k1_l)
        dw_pick = pick_words("dw_pick", dw_tab, k1_l)
        ds = deal("ds", ds_pick, U8, 1)
        dw = deal("dw", dw_pick, I32, 1)
        for e in range(2):
            nc.sync.dma_start(ds[2 + e : P : 32, :].bitcast(I32), ds[16 + e : P : 32, :].bitcast(I32))

        ex_win = [sb("ex_win%d" % t, [P, 2 * S], F32) for t in range(PACK)]
        d_g, y_g = [], []
        for t in range(PACK):
            nc.scalar.activation(ex_win[t][:, S : S + HALF], d_banks[t][:, :HALF], ACT.Tanh)
            d_g.append(sb("d_g%d" % t, [P, S], F32))
            nc.scalar.activation(d_g[t][:], d_banks[t][:], ACT.Copy, scale=gain[:, t : t + 1])
        for t in range(PACK):
            y_g.append(sb("y_g%d" % t, [P, S], F32))
            nc.scalar.activation(y_g[t][:], y_banks[t][:], ACT.Copy, scale=gain[:, t : t + 1])
        for t in range(PACK):
            nc.scalar.activation(ex_win[t][:, S + HALF :], d_banks[t][:, HALF:], ACT.Tanh)

        half_h = [sb("half_h%d" % t, [P, S], F32) for t in range(PACK)]
        ex_own = [sb("ex_own%d" % t, [P, S], F32) for t in range(PACK)]
        held_copies = []
        gap_copies = []
        late_copies = [[] for t in range(PACK)]
        for c, (c0, c1) in enumerate(Z_CHUNKS):
            width = c1 - c0
            if c0 % HALF == 0:
                half0 = c0
                prod = [sb("prod%d_%d" % (c0, t), [P, HALF], F32)[:] for t in range(PACK - 2 * (c > 0))]
                if c > 0:
                    prod.extend([z[:, 2, :], z[:, 3, :]])
                for t in range(PACK):
                    nc.vector.tensor_tensor(
                        prod[t],
                        d_g[t][:].indirect(part(n2_l, c0, c0 + HALF)),
                        ex_win[t][:, S + c0 : S + c0 + HALF],
                        ALU.mult,
                    )
            if c < 2:
                z_tile = sb("z%d" % c, [P, PACK + 3 * c, width], F32)
            z = z_tile[:, 3:, :] if c == 2 else z_tile[:, :PACK, :]
            for t in (1, 2, 3, 0) if c == 2 else range(PACK):
                nc.vector.tensor_tensor(
                    z[:, t, :], y_g[t][:].indirect(part(n1_l, c0, c1)), prod[t][:, c0 - half0 : c1 - half0], ALU.subtract
                )
            z_bf = sb("z_bf%d" % c, [P, width, PACK], BF16)
            weave(nc.scalar.copy if c < 2 else nc.vector.tensor_copy, z_bf, z)
            for dst, src in held_copies:
                nc.scalar.activation(dst, src, ACT.Copy, scale=0.03125)
            held_copies = []
            z_words = sb("z_words%d" % c, [P, width], I32)
            nc.vector.quantize_mx(z_words[:].bitcast(FP8X4), z_scales[:, c0:c1], z_bf[:].rearrange("p j t -> p (j t)"))
            for dst, src in gap_copies:
                nc.vector.tensor_scalar_mul(dst, src, 0.03125)
            h_banks = []
            for t in range(PACK):
                bank = psum.tile([P, S], F32, name="bank", tag="bank%d" % (PACK * ((c + 1) % 2) + t))
                nc.tensor.matmul_mx(
                    bank[:, :width],
                    lhsT=dw[:, P * t : P * (t + 1)].bitcast(FP8X4),
                    lhsT_scale=ds[:, P * t : P * (t + 1)],
                    rhs=z_words[:].bitcast(FP8X4),
                    rhs_scale=z_scales[:, c0:c1],
                    start=True,
                    stop=True,
                )
                h_banks.append(bank)
            for t in range(PACK):
                nc.scalar.activation(ex_win[t][:, c0:c1], h_banks[t][:, :width], ACT.Exp, scale=0.03125)
                nc.sync.dma_start(ex_own[t][:, c0:c1], ex_win[t][:, c0:c1])
            for t in range(PACK):
                if c == 2:
                    late_copies[t].append((half_h[t][:, c0:c1], h_banks[t][:, :width]))
                elif c == 1:
                    gap_copies.append((half_h[t][:, c0:c1], h_banks[t][:, :width]))
                elif t > 0:
                    held_copies.append((half_h[t][:, c0:c1], h_banks[t][:, :width]))
                else:
                    nc.scalar.activation(half_h[t][:, c0:c1], h_banks[t][:, :width], ACT.Copy, scale=0.03125)

        ex4 = [sb("ex4_%d" % t, [P, S], F32) for t in range(PACK)]
        for t in range(PACK):
            for dst, src in late_copies[t]:
                nc.scalar.activation(dst, src, ACT.Copy, scale=0.03125)
            for c0 in (0, HALF):
                nc.scalar.activation(ex4[t][:, c0 : c0 + HALF], half_h[t][:].indirect(part(n4_l, c0, c0 + HALF)), ACT.Exp)

        num = [sb("num0", [P, PACK, HALF], F32), sb("num1", [P, PACK, HALF], F32, "half_h2")]
        den = sb("den", [P, PACK, S], F32)

        def numerator(t, c0):
            nc.vector.tensor_tensor(
                num[c0 // HALF][:, t, :],
                ex_win[t][:].indirect(part(n3_l, c0, c0 + HALF)),
                ex_own[t][:, c0 : c0 + HALF],
                ALU.add,
            )

        for t in range(PACK):
            numerator(t, 0)
        for t in range(PACK):
            nc.vector.tensor_tensor(den[:, t, :], ex_win[t][:].indirect(n5_l[:]), ex4[t][:], ALU.add)
        for t in range(PACK):
            numerator(t, HALF)

        out_rows = out_0.rearrange("(p t) j -> p t j", t=PACK)
        o_scales = sb("o_scales", [P, S], U8)
        log_num = [sb("log_num0", [P, PACK, HALF], F32, "half_h3"), sb("log_num1", [P, PACK, HALF], F32)]
        log_den = [sb("log_den%d" % h, [P, PACK, HALF], F32) for h in range(2)]
        nc.scalar.activation(log_num[0][:], num[0][:], ACT.Ln)
        for h in range(2):
            nc.scalar.activation(log_den[h][:], den[:, :, h * HALF : (h + 1) * HALF], ACT.Ln)
        for a in (0, QUARTER):
            nc.scalar.activation(log_num[1][:, :, a : a + QUARTER], num[1][:, :, a : a + QUARTER], ACT.Ln)
        res = [sb("res%d" % i, [P, PACK, QUARTER], F32) for i in range(4)]
        o_bf = [sb("o_bf%d" % i, [P, QUARTER, PACK], BF16) for i in range(4)]
        o_words = [sb("o_words%d" % h, [P, HALF], I32) for h in range(2)]

        def difference(i):
            h, a = i // 2, i % 2 * QUARTER
            nc.vector.tensor_tensor(
                res[i][:], log_num[h][:, :, a : a + QUARTER], log_den[h][:, :, a : a + QUARTER], ALU.subtract
            )
            nc.sync.dma_start(out_rows[:, :, i * QUARTER : (i + 1) * QUARTER], res[i][:])

        def quantise(i):
            h, a = i // 2, i % 2 * QUARTER
            nc.vector.quantize_mx(
                o_words[h][:, a : a + QUARTER].bitcast(FP8X4),
                o_scales[:, i * QUARTER : (i + 1) * QUARTER],
                o_bf[i][:].rearrange("p j t -> p (j t)"),
            )
            if a:
                words_out = out_1[0, :, h * HALF : (h + 1) * HALF, :].rearrange("p c r -> p (c r)")
                nc.sync.dma_start(words_out.bitcast(I32), o_words[h][:])

        difference(0)
        difference(1)
        weave(nc.vector.tensor_copy, o_bf[0], res[0][:])
        difference(2)
        quantise(0)
        difference(3)
        weave(nc.scalar.copy, o_bf[1], res[1][:])
        weave(nc.scalar.copy, o_bf[2], res[2][:])
        quantise(1)
        weave(nc.vector.tensor_copy, o_bf[3], res[3][:])
        quantise(2)
        quantise(3)
        for q in range(4):
            queue = nc.sync if q == 0 else nc.scalar
            queue.dma_start(out_2[0, 4 * q : 4 * q + 4, :].bitcast(I32), o_scales[32 * q : 32 * q + 4, :].bitcast(I32))
